import numpy as np
import ml_dtypes


def mxq(x, axis, fmt="e4m3"):
    dtype, down = {"e4m3": (ml_dtypes.float8_e4m3fn, 7), "e5m2": (ml_dtypes.float8_e5m2, 14)}[fmt]
    v = np.moveaxis(np.asarray(x, np.float32).astype(ml_dtypes.bfloat16).astype(np.float64), axis, -1)
    blocks = v.reshape(v.shape[:-1] + (-1, 32))
    amax = np.abs(blocks).max(-1, keepdims=True)
    byte = np.maximum(np.where(amax > 0, np.frexp(amax)[1] - 1 + 127, 0) - down, 1)
    scale = np.exp2(byte - 127.0)
    codes = (blocks / scale).astype(np.float32).astype(dtype).astype(np.float64)
    return np.moveaxis((codes * scale).reshape(v.shape), -1, axis)


WIDE = False


def mx_kscale(k):
    if not WIDE:
        return np.ones(k)
    levels = np.array([10, -10, 5, -5, 0])
    if k % 512:
        return np.exp2(np.random.permutation(np.resize(levels, k // 32))).repeat(32)
    a = np.empty((k // 512, 16))
    for p in range(k // 512):
        a[p, :8] = np.random.permutation(np.resize(levels, 8))
        for g in range(8):
            far = levels[np.abs(levels - a[p, g]) >= 10]
            a[p, g + 8] = far[np.random.randint(len(far))]
    return np.exp2(a.ravel()).repeat(32)


BF16 = ml_dtypes.bfloat16


def bf(x):
    return np.asarray(x, np.float32).astype(BF16)


def f64(x):
    return np.asarray(x).astype(np.float64)


E2M1 = np.array([0.0, 0.5, 1.0, 1.5, 2.0, 3.0, 4.0, 6.0, -0.0, -0.5, -1.0, -1.5, -2.0, -3.0, -4.0, -6.0])


def pack_weight(w, fmt):
    k, n = w.shape
    w = f64(bf(w)).reshape(k // 32, 32, n)
    amax = np.abs(w).max(1)
    if fmt == "e4m3":
        byte = np.frexp(amax)[1] - 1 + 127 - 7
    else:
        mant, ex = np.frexp(amax / 6.0)
        byte = np.where(mant > 0.5, ex, ex - 1) + 127
    byte = np.clip(np.where(amax > 0, byte, 1), 1, 254)
    scaled = (w * np.exp2(127.0 - byte)[:, None, :]).reshape(k, n).astype(np.float32)
    by_word = np.ascontiguousarray(scaled.reshape(k // 512, 128, 4, n).transpose(0, 1, 3, 2))
    if fmt == "e4m3":
        words = by_word.astype(ml_dtypes.float8_e4m3fn).view(np.uint8)
    else:
        c = by_word.astype(ml_dtypes.float4_e2m1fn).view(np.uint8) & 0xF
        words = c[..., 0::2] | (c[..., 1::2] << 4)
    return np.ascontiguousarray(words), np.ascontiguousarray(byte.astype(np.uint8).reshape(k // 512, 16, n))


def unpack_weight(words, scales, fmt):
    g, p, n, _ = words.shape
    if fmt == "e4m3":
        vals = np.ascontiguousarray(words).view(ml_dtypes.float8_e4m3fn).astype(np.float64)
    else:
        nib = np.empty((g, p, n, 4), np.uint8)
        nib[..., 0::2] = words & 0xF
        nib[..., 1::2] = words >> 4
        vals = E2M1[nib]
    vals = vals * np.repeat(np.exp2(scales.astype(np.float64) - 127.0), 8, axis=1)[..., None]
    return vals.transpose(0, 1, 3, 2).reshape(g * 512, n)
def pack4(w):
    words, scales = pack_weight(w, "e2m1")
    return words.reshape(words.shape[0], 128, -1), scales


def unpack4(words, scales):
    return unpack_weight(words.reshape(words.shape[0], 128, -1, 2), scales, "e2m1")


def planes(Y):
    n, m = Y.shape
    b = f64(bf(Y)).reshape(n // 32, 32, m)
    amax = np.abs(b).max(1)
    byte = np.clip(np.where(amax > 0, np.frexp(amax)[1] - 1 + 127 - 7, 1), 1, 254)
    codes = (b * np.exp2(127.0 - byte)[:, None, :]).reshape(n, m).astype(np.float32).astype(ml_dtypes.float8_e4m3fn).view(np.uint8)
    words = codes.reshape(n // 512, 128, 4, m).transpose(0, 1, 3, 2)
    return np.ascontiguousarray(words), np.ascontiguousarray(byte.astype(np.uint8).reshape(n // 512, 16, m))


S, E, T, L = 1024, 2048, 1536, 768

def setup_inputs():
    s = mx_kscale(S)
    t = mx_kscale(E)
    C = np.random.randn(S, E) / np.sqrt(S) / s[:, None]
    B = np.random.randn(S, L) * s[:, None]
    c_words, c_scales = pack4(C)
    b_words, b_scales = pack4(B)
    att = np.exp(-np.abs(0.7 * np.random.randn(E))) * t
    offset = 0.3 * np.random.randn(E) * t
    recode = 1.5 * np.random.randn(T, E) / np.sqrt(E) / t[None, :]
    local = 0.5 * np.random.randn(T, L)
    power = np.exp(0.8 * np.random.randn(T))
    return {"c_words": c_words, "c_scales": c_scales,
            "b_words": b_words, "b_scales": b_scales,
            "att": bf(att), "offset": bf(offset), "recode": bf(recode),
            "local": bf(local), "power": bf(power)}

def reference(c_words, c_scales, b_words, b_scales, att, offset, recode, local, power):
    C = unpack4(c_words, c_scales)
    B = unpack4(b_words, b_scales)
    coded = C.T @ B
    received = f64(att)[:, None] * coded + f64(offset)[:, None]
    mix = mxq(f64(recode), 1, "e4m3") @ mxq(received, 0, "e4m3")
    y = f64(power)[:, None] * np.tanh(mix + f64(local))
    Y = y.reshape(T, L)
    words, scales = planes(Y)
    return y, words, scales

@@ -1,0 +1,346 @@
+from contextlib import ExitStack
+
+import concourse.mybir as mybir
+from concourse.masks import make_identity
+
+S, E, T, L = 1024, 2048, 1536, 768
+FLOPS = 2 * S * E * L + 2 * T * E * L
+
+F32 = mybir.dt.float32
+BF16 = mybir.dt.bfloat16
+I32 = mybir.dt.int32
+U32 = mybir.dt.uint32
+U8 = mybir.dt.uint8
+FP8X4 = mybir.dt.float8_e4m3fn_x4
+FP4X4 = mybir.dt.float4_e2m1fn_x4
+ACT = mybir.ActivationFunctionType
+ALU = mybir.AluOpType
+
+P = 128
+PACK = 4
+K_PASS = P * PACK
+S_PASSES = S // K_PASS
+E_GROUPS = E // K_PASS
+T_GROUPS = T // K_PASS
+CHUNK = 256
+CHUNKS = L // CHUNK
+BANK = 512
+
+
+def tile_coded_relay_recode_k5_kernel(
+    tc, c_words, c_scales, b_words, b_scales, att, offset, recode, local, power, out_0, out_1, out_2
+):
+    nc = tc.nc
+    with ExitStack() as ctx:
+        keep = ctx.enter_context(tc.tile_pool(name="keep", bufs=1))
+        raw_pool = ctx.enter_context(tc.tile_pool(name="raw", bufs=8))
+        work = ctx.enter_context(tc.tile_pool(name="work", bufs=2))
+        ring = ctx.enter_context(tc.tile_pool(name="ring", bufs=4))
+        psum = ctx.enter_context(tc.psum_pool(name="psum", bufs=8))
+        ctx.enter_context(tc.manual_schedule())
+
+        def kept(name, shape, dtype):
+            return keep.tile(shape, dtype, name=name, align_bytes=64)
+
+        ident = kept("ident", [P, P], F32)
+        warm = kept("warm", [P, 1], F32)
+        cw_raw = [kept("cw_raw%d" % e, [P, S_PASSES, 2 * K_PASS], U8) for e in range(E_GROUPS)]
+        cw = [kept("cw%d" % e, [P, S_PASSES, PACK, 2 * P], U8) for e in range(E_GROUPS)]
+        cs_first = kept("cs_first", [P, S_PASSES, K_PASS], U8)
+        cs_rest = kept("cs_rest", [P, S_PASSES, E - K_PASS], U8)
+        cs = [kept("cs%d" % e, [P, S_PASSES, PACK, P], U8) for e in range(E_GROUPS)]
+        bw = kept("bw", [P, S_PASSES, 2 * L], U8)
+        bs = kept("bs", [P, S_PASSES, L], U8)
+        att_b = kept("att_b", [P, E_GROUPS, PACK], BF16)
+        off_b = kept("off_b", [P, E_GROUPS, PACK], BF16)
+        pow_b = kept("pow_b", [P, T_GROUPS, PACK], BF16)
+        att_f = kept("att_f", [P, E_GROUPS, PACK], F32)
+        off_f = kept("off_f", [P, E_GROUPS, PACK], F32)
+        pow_f = kept("pow_f", [P, T_GROUPS, PACK], F32)
+        loc = [kept("loc%d" % g, [P, PACK, L], BF16) for g in range(T_GROUPS)]
+        rx_codes = [kept("rx_codes%d" % e, [P, L], U32) for e in range(E_GROUPS)]
+        rx_scales = [kept("rx_scales%d" % e, [P, L], U8) for e in range(E_GROUPS)]
+        w_codes = [kept("w_codes%d" % i, [P, E_GROUPS * P], U32) for i in range(T_GROUPS * PACK)]
+        w_scales = [kept("w_scales%d" % i, [P, E_GROUPS * P], U8) for i in range(T_GROUPS * PACK)]
+        y_codes = [kept("y_codes%d" % g, [P, L], U32) for g in range(T_GROUPS)]
+        y_scales = [kept("y_scales%d" % g, [P, L], U8) for g in range(T_GROUPS)]
+
+        w_raw = {}
+        w_grouped = {}
+        rx_rows = {}
+        rx_grouped = {}
+        mix_bank = {}
+        z_half = {}
+        y_unit = {}
+        y_grouped = {}
+
+        def new_bank():
+            return psum.tile([P, BANK], F32, name="bank")
+
+        def load_scale_rows(plane, rows):
+            for q in range(4):
+                nc.sync.dma_start(
+                    out=plane[32 * q : 32 * q + 4, :, :].bitcast(I32),
+                    in_=rows[:, 4 * q : 4 * q + 4, :].rearrange("g r n -> r g n").bitcast(I32),
+                )
+
+        def load_c_words(e):
+            nc.sync.dma_start(
+                out=cw_raw[e][:].bitcast(I32),
+                in_=c_words[:, :, 2 * K_PASS * e : 2 * K_PASS * (e + 1)].rearrange("g p n -> p g n").bitcast(I32),
+            )
+
+        def load_recode(i):
+            g, j = divmod(i, PACK)
+            w_raw[i] = raw_pool.tile([P, E], BF16, name="w_raw", align_bytes=64)
+            rows = recode[K_PASS * g : K_PASS * (g + 1), :].rearrange("(m j) k -> m j k", j=PACK)
+            nc.sync.dma_start(out=w_raw[i][:], in_=rows[:, j, :])
+
+        def load_local(g):
+            nc.sync.dma_start(
+                out=loc[g][:], in_=local[K_PASS * g : K_PASS * (g + 1), :].rearrange("(p t) l -> p t l", t=PACK)
+            )
+
+        def load_vector(dst_b, dst_f, vec):
+            nc.sync.dma_start(out=dst_b[:], in_=vec.rearrange("(g p t) -> p g t", p=P, t=PACK))
+            nc.gpsimd.tensor_copy(out=dst_f[:], in_=dst_b[:])
+
+        def order_c_words(e):
+            nc.vector.tensor_copy(
+                out=cw[e][:].rearrange("p g t (m b) -> p g t m b", b=2),
+                in_=cw_raw[e][:].rearrange("p g (m t b) -> p g t m b", t=PACK, b=2),
+            )
+
+        def order_c_scales(e):
+            src = cs_first[:] if e == 0 else cs_rest[:, :, K_PASS * (e - 1) : K_PASS * e]
+            nc.vector.tensor_copy(out=cs[e][:], in_=src.rearrange("p g (m t) -> p g t m", t=PACK))
+
+        def turn_recode(i):
+            words = w_raw[i][:].bitcast(F32)
+            w_grouped[i] = ring.tile([P, E_GROUPS, P, PACK], BF16, name="w_grouped", align_bytes=64)
+            pairs = w_grouped[i][:].bitcast(F32)
+            for h in range(2):
+                bank = new_bank()
+                for a in range(2):
+                    e = 2 * h + a
+                    for u in range(2):
+                        col = (2 * a + u) * P
+                        nc.tensor.transpose(
+                            bank[:, col : col + P], words[:, 2 * P * e + u : 2 * P * (e + 1) : 2], ident[:]
+                        )
+                nc.scalar.copy(
+                    out=pairs[:, 2 * h : 2 * h + 2, :, :],
+                    in_=bank[:].rearrange("p (a u m) -> p a m u", a=2, u=2),
+                )
+
+        def quantize_recode(i):
+            nc.vector.quantize_mx(
+                out=w_codes[i][:].bitcast(FP8X4),
+                scales=w_scales[i][:],
+                in_=w_grouped[i][:].rearrange("p e m t -> p (e m t)"),
+            )
+
+        def coded_passes(out, e, t, lo, hi):
+            for g in range(S_PASSES):
+                nc.tensor.matmul_mx(
+                    out=out,
+                    lhsT=cw[e][:, g, t, :].bitcast(FP4X4),
+                    lhsT_scale=cs[e][:, g, t, :],
+                    rhs=bw[:, g, 2 * lo : 2 * hi].bitcast(FP4X4),
+                    rhs_scale=bs[:, g, lo:hi],
+                    start=(g == 0),
+                    stop=(g == S_PASSES - 1),
+                )
+
+        def receive(src, e, t, lo, hi):
+            nc.scalar.activation(
+                out=rx_rows[e][:, t, lo:hi],
+                in_=src,
+                func=ACT.Identity,
+                bias=off_f[:, e, t : t + 1],
+                scale=att_f[:, e, t : t + 1],
+            )
+
+        def code_pair(e, h):
+            if h == 0:
+                rx_rows[e] = work.tile([P, PACK, L], BF16, name="rx_rows", align_bytes=64)
+            t0, t1 = 2 * h, 2 * h + 1
+            rest = L - BANK
+            first = new_bank()
+            coded_passes(first[:], e, t0, 0, BANK)
+            receive(first[:], e, t0, 0, BANK)
+            second = new_bank()
+            coded_passes(second[:], e, t1, 0, BANK)
+            receive(second[:], e, t1, 0, BANK)
+            shared = new_bank()
+            coded_passes(shared[:, 0:rest], e, t0, BANK, L)
+            coded_passes(shared[:, rest : 2 * rest], e, t1, BANK, L)
+            receive(shared[:, 0:rest], e, t0, BANK, L)
+            receive(shared[:, rest : 2 * rest], e, t1, BANK, L)
+
+        def interleave(dst, src):
+            nc.vector.tensor_copy(
+                out=dst.rearrange("p (c i) t -> p c t i", i=4), in_=src.rearrange("p t (c i) -> p c t i", i=4)
+            )
+
+        def group_received(e, c):
+            rx_grouped[e, c] = ring.tile([P, CHUNK, PACK], BF16, name="rx_grouped", align_bytes=64)
+            interleave(rx_grouped[e, c][:], rx_rows[e][:, :, CHUNK * c : CHUNK * (c + 1)])
+
+        def quantize_received(e, c):
+            cols = slice(CHUNK * c, CHUNK * (c + 1))
+            nc.vector.quantize_mx(
+                out=rx_codes[e][:, cols].bitcast(FP8X4),
+                scales=rx_scales[e][:, cols],
+                in_=rx_grouped[e, c][:].rearrange("p l t -> p (l t)"),
+            )
+
+        def half_of(n):
+            unit, h = divmod(n, 2)
+            g, c = divmod(unit, CHUNKS)
+            return unit, g, slice(CHUNK * c, CHUNK * (c + 1)), h
+
+        def mix(n):
+            unit, g, cols, h = half_of(n)
+            mix_bank[n] = new_bank()
+            for a in range(2):
+                i = PACK * g + 2 * h + a
+                for e in range(E_GROUPS):
+                    nc.tensor.matmul_mx(
+                        out=mix_bank[n][:, CHUNK * a : CHUNK * (a + 1)],
+                        lhsT=w_codes[i][:, P * e : P * (e + 1)].bitcast(FP8X4),
+                        lhsT_scale=w_scales[i][:, P * e : P * (e + 1)],
+                        rhs=rx_codes[e][:, cols].bitcast(FP8X4),
+                        rhs_scale=rx_scales[e][:, cols],
+                        start=(e == 0),
+                        stop=(e == E_GROUPS - 1),
+                    )
+
+        def add_local(n):
+            unit, g, cols, h = half_of(n)
+            z_half[n] = ring.tile([P, 2, CHUNK], F32, name="z_half")
+            nc.vector.tensor_tensor(
+                out=z_half[n][:],
+                in0=mix_bank[n][:].rearrange("p (a l) -> p a l", a=2),
+                in1=loc[g][:, 2 * h : 2 * h + 2, cols],
+                op=ALU.add,
+            )
+
+        def limit(n):
+            nc.scalar.activation(out=z_half[n][:], in_=z_half[n][:], func=ACT.Tanh)
+
+        def amplify(n):
+            unit, g, cols, h = half_of(n)
+            if h == 0:
+                y_unit[unit] = ring.tile([P, PACK, CHUNK], F32, name="y_unit")
+            for a in range(2):
+                t = 2 * h + a
+                nc.scalar.activation(
+                    out=y_unit[unit][:, t, :], in_=z_half[n][:, a, :], func=ACT.Copy, scale=pow_f[:, g, t : t + 1]
+                )
+            if h == 1:
+                rows = out_0[K_PASS * g : K_PASS * (g + 1), cols].rearrange("(p t) l -> p t l", t=PACK)
+                nc.sync.dma_start(out=rows, in_=y_unit[unit][:])
+
+        def group_y(unit):
+            y_grouped[unit] = work.tile([P, CHUNK, PACK], BF16, name="y_grouped", align_bytes=64)
+            interleave(y_grouped[unit][:], y_unit[unit][:])
+
+        def quantize_y(unit):
+            g, c = divmod(unit, CHUNKS)
+            cols = slice(CHUNK * c, CHUNK * (c + 1))
+            nc.vector.quantize_mx(
+                out=y_codes[g][:, cols].bitcast(FP8X4),
+                scales=y_scales[g][:, cols],
+                in_=y_grouped[unit][:].rearrange("p l t -> p (l t)"),
+            )
+            words = out_1[g].rearrange("p m t -> p (m t)").bitcast(I32)
+            nc.sync.dma_start(out=words[:, cols], in_=y_codes[g][:, cols].bitcast(I32))
+            if c == CHUNKS - 1:
+                for q in range(4):
+                    nc.sync.dma_start(
+                        out=out_2[g, 4 * q : 4 * q + 4, :].bitcast(I32),
+                        in_=y_scales[g][32 * q : 32 * q + 4, :].bitcast(I32),
+                    )
+
+        nc.vector.memset(cs_first[:].bitcast(I32), 0)
+        nc.vector.memset(bs[:].bitcast(I32), 0)
+        nc.vector.memset(cs_rest[:].bitcast(I32), 0)
+        nc.vector.memset(warm[:], 0.0)
+        nc.scalar.activation(out=warm[:], in_=warm[:], func=ACT.Tanh)
+        make_identity(nc, ident[:])
+        load_c_words(0)
+        nc.sync.dma_start(out=bw[:].bitcast(I32), in_=b_words.rearrange("g p n -> p g n").bitcast(I32))
+        load_scale_rows(cs_first, c_scales[:, :, 0:K_PASS])
+        load_scale_rows(bs, b_scales)
+        load_recode(0)
+        load_vector(att_b, att_f, att)
+        load_vector(off_b, off_f, offset)
+        load_recode(1)
+        load_scale_rows(cs_rest, c_scales[:, :, K_PASS:E])
+        load_c_words(1)
+        load_recode(2)
+        load_c_words(2)
+        load_recode(3)
+        load_c_words(3)
+        for i in range(4, 8):
+            load_recode(i)
+
+        order_c_words(0)
+        order_c_scales(0)
+        code_pair(0, 0)
+        turn_recode(0)
+        load_recode(8)
+        order_c_words(1)
+        order_c_scales(1)
+        code_pair(0, 1)
+        turn_recode(1)
+        load_recode(9)
+        load_vector(pow_b, pow_f, power)
+        load_local(0)
+        quantize_recode(0)
+        order_c_words(2)
+        order_c_scales(2)
+        for e in range(1, E_GROUPS + 1):
+            a, b, d = 3 * e - 1, 3 * e, 3 * e + 1
+            if e < E_GROUPS:
+                code_pair(e, 0)
+            turn_recode(a)
+            if e == 1:
+                load_recode(10)
+            group_received(e - 1, 0)
+            group_received(e - 1, 1)
+            quantize_received(e - 1, 0)
+            quantize_recode(a - 1)
+            quantize_received(e - 1, 1)
+            group_received(e - 1, 2)
+            if e < E_GROUPS:
+                turn_recode(b)
+                if e == 1:
+                    load_recode(11)
+                    load_local(1)
+                    load_local(2)
+                quantize_recode(a)
+                quantize_received(e - 1, 2)
+                code_pair(e, 1)
+                if e == 1:
+                    order_c_words(3)
+                    order_c_scales(3)
+                quantize_recode(b)
+                turn_recode(d)
+            else:
+                quantize_recode(a)
+                quantize_received(e - 1, 2)
+
+        halves = 2 * T_GROUPS * CHUNKS
+        for n in range(halves + 5):
+            if n < halves:
+                mix(n)
+                add_local(n)
+                limit(n)
+            if 1 <= n <= halves:
+                amplify(n - 1)
+            if n % 2 == 1 and 3 <= n < halves + 3:
+                group_y((n - 3) // 2)
+            if n % 2 == 0 and 4 <= n < halves + 4:
+                quantize_y((n - 4) // 2)

@@ -25,6 +25,8 @@ T_GROUPS = T // K_PASS
 CHUNK = 256
 CHUNKS = L // CHUNK
 BANK = 512
+UNITS = [(g, CHUNK * c, CHUNK) for g in range(T_GROUPS) for c in range(CHUNKS)][:-1]
+UNITS = UNITS + [(T_GROUPS - 1, L - CHUNK, P), (T_GROUPS - 1, L - P, P)]
 
 
 def tile_coded_relay_recode_k5_kernel(
@@ -46,8 +48,7 @@ def tile_coded_relay_recode_k5_kernel(
         warm = kept("warm", [P, 1], F32)
         cw_raw = [kept("cw_raw%d" % e, [P, S_PASSES, 2 * K_PASS], U8) for e in range(E_GROUPS)]
         cw = [kept("cw%d" % e, [P, S_PASSES, PACK, 2 * P], U8) for e in range(E_GROUPS)]
-        cs_first = kept("cs_first", [P, S_PASSES, K_PASS], U8)
-        cs_rest = kept("cs_rest", [P, S_PASSES, E - K_PASS], U8)
+        cs_raw = kept("cs_raw", [P, S_PASSES, E], U8)
         cs = [kept("cs%d" % e, [P, S_PASSES, PACK, P], U8) for e in range(E_GROUPS)]
         bw = kept("bw", [P, S_PASSES, 2 * L], U8)
         bs = kept("bs", [P, S_PASSES, L], U8)
@@ -63,8 +64,9 @@ def tile_coded_relay_recode_k5_kernel(
         w_codes = [kept("w_codes%d" % i, [P, E_GROUPS * P], U32) for i in range(T_GROUPS * PACK)]
         w_scales = [kept("w_scales%d" % i, [P, E_GROUPS * P], U8) for i in range(T_GROUPS * PACK)]
         y_codes = [kept("y_codes%d" % g, [P, L], U32) for g in range(T_GROUPS)]
-        y_scales = [kept("y_scales%d" % g, [P, L], U8) for g in range(T_GROUPS)]
+        y_scales = kept("y_scales", [P, T_GROUPS, L], U8)
 
+        turned = {}
         w_raw = {}
         w_grouped = {}
         rx_rows = {}
@@ -77,9 +79,9 @@ def tile_coded_relay_recode_k5_kernel(
         def new_bank():
             return psum.tile([P, BANK], F32, name="bank")
 
-        def load_scale_rows(plane, rows):
+        def load_scale_rows(queue, plane, rows):
             for q in range(4):
-                nc.sync.dma_start(
+                queue.dma_start(
                     out=plane[32 * q : 32 * q + 4, :, :].bitcast(I32),
                     in_=rows[:, 4 * q : 4 * q + 4, :].rearrange("g r n -> r g n").bitcast(I32),
                 )
@@ -90,11 +92,14 @@ def tile_coded_relay_recode_k5_kernel(
                 in_=c_words[:, :, 2 * K_PASS * e : 2 * K_PASS * (e + 1)].rearrange("g p n -> p g n").bitcast(I32),
             )
 
-        def load_recode(i):
+        def load_recode(i, parts=1):
             g, j = divmod(i, PACK)
             w_raw[i] = raw_pool.tile([P, E], BF16, name="w_raw", align_bytes=64)
             rows = recode[K_PASS * g : K_PASS * (g + 1), :].rearrange("(m j) k -> m j k", j=PACK)
-            nc.sync.dma_start(out=w_raw[i][:], in_=rows[:, j, :])
+            width = E // parts
+            for a in range(parts):
+                cols = slice(width * a, width * (a + 1))
+                nc.sync.dma_start(out=w_raw[i][:, cols], in_=rows[:, j, cols])
 
         def load_local(g):
             nc.sync.dma_start(
@@ -112,13 +117,11 @@ def tile_coded_relay_recode_k5_kernel(
             )
 
         def order_c_scales(e):
-            src = cs_first[:] if e == 0 else cs_rest[:, :, K_PASS * (e - 1) : K_PASS * e]
+            src = cs_raw[:, :, K_PASS * e : K_PASS * (e + 1)]
             nc.vector.tensor_copy(out=cs[e][:], in_=src.rearrange("p g (m t) -> p g t m", t=PACK))
 
         def turn_recode(i):
             words = w_raw[i][:].bitcast(F32)
-            w_grouped[i] = ring.tile([P, E_GROUPS, P, PACK], BF16, name="w_grouped", align_bytes=64)
-            pairs = w_grouped[i][:].bitcast(F32)
             for h in range(2):
                 bank = new_bank()
                 for a in range(2):
@@ -128,10 +131,17 @@ def tile_coded_relay_recode_k5_kernel(
                         nc.tensor.transpose(
                             bank[:, col : col + P], words[:, 2 * P * e + u : 2 * P * (e + 1) : 2], ident[:]
                         )
-                nc.scalar.copy(
-                    out=pairs[:, 2 * h : 2 * h + 2, :, :],
-                    in_=bank[:].rearrange("p (a u m) -> p a m u", a=2, u=2),
-                )
+                turned[i, h] = bank
+
+        def empty_turned(i, h, on_vector):
+            if h == 0:
+                w_grouped[i] = ring.tile([P, E_GROUPS, P, PACK], BF16, name="w_grouped", align_bytes=64)
+            dst = w_grouped[i][:].bitcast(F32)[:, 2 * h : 2 * h + 2, :, :]
+            src = turned[i, h][:].rearrange("p (a u m) -> p a m u", a=2, u=2)
+            if on_vector:
+                nc.vector.tensor_copy(out=dst, in_=src)
+            else:
+                nc.scalar.copy(out=dst, in_=src)
 
         def quantize_recode(i):
             nc.vector.quantize_mx(
@@ -197,31 +207,35 @@ def tile_coded_relay_recode_k5_kernel(
 
         def half_of(n):
             unit, h = divmod(n, 2)
-            g, c = divmod(unit, CHUNKS)
-            return unit, g, slice(CHUNK * c, CHUNK * (c + 1)), h
+            g, lo, width = UNITS[unit]
+            return unit, g, slice(lo, lo + width), h, width
+
+        def mix_passes(out, i, cols):
+            for e in range(E_GROUPS):
+                nc.tensor.matmul_mx(
+                    out=out,
+                    lhsT=w_codes[i][:, P * e : P * (e + 1)].bitcast(FP8X4),
+                    lhsT_scale=w_scales[i][:, P * e : P * (e + 1)],
+                    rhs=rx_codes[e][:, cols].bitcast(FP8X4),
+                    rhs_scale=rx_scales[e][:, cols],
+                    start=(e == 0),
+                    stop=(e == E_GROUPS - 1),
+                )
 
         def mix(n):
-            unit, g, cols, h = half_of(n)
+            unit, g, cols, h, width = half_of(n)
             mix_bank[n] = new_bank()
             for a in range(2):
-                i = PACK * g + 2 * h + a
-                for e in range(E_GROUPS):
-                    nc.tensor.matmul_mx(
-                        out=mix_bank[n][:, CHUNK * a : CHUNK * (a + 1)],
-                        lhsT=w_codes[i][:, P * e : P * (e + 1)].bitcast(FP8X4),
-                        lhsT_scale=w_scales[i][:, P * e : P * (e + 1)],
-                        rhs=rx_codes[e][:, cols].bitcast(FP8X4),
-                        rhs_scale=rx_scales[e][:, cols],
-                        start=(e == 0),
-                        stop=(e == E_GROUPS - 1),
-                    )
+                mix_passes(mix_bank[n][:, width * a : width * (a + 1)], PACK * g + 2 * h + a, cols)
 
         def add_local(n):
-            unit, g, cols, h = half_of(n)
-            z_half[n] = ring.tile([P, 2, CHUNK], F32, name="z_half")
+            unit, g, cols, h, width = half_of(n)
+            if h == 0:
+                y_unit[unit] = ring.tile([P, PACK, width], F32, name="y_unit")
+            z_half[n] = ring.tile([P, 2, width], F32, name="z_half", bufs=6)
             nc.vector.tensor_tensor(
                 out=z_half[n][:],
-                in0=mix_bank[n][:].rearrange("p (a l) -> p a l", a=2),
+                in0=mix_bank[n][:, 0 : 2 * width].rearrange("p (a l) -> p a l", a=2),
                 in1=loc[g][:, 2 * h : 2 * h + 2, cols],
                 op=ALU.add,
             )
@@ -229,118 +243,313 @@ def tile_coded_relay_recode_k5_kernel(
         def limit(n):
             nc.scalar.activation(out=z_half[n][:], in_=z_half[n][:], func=ACT.Tanh)
 
-        def amplify(n):
-            unit, g, cols, h = half_of(n)
-            if h == 0:
-                y_unit[unit] = ring.tile([P, PACK, CHUNK], F32, name="y_unit")
-            for a in range(2):
-                t = 2 * h + a
-                nc.scalar.activation(
-                    out=y_unit[unit][:, t, :], in_=z_half[n][:, a, :], func=ACT.Copy, scale=pow_f[:, g, t : t + 1]
-                )
-            if h == 1:
-                rows = out_0[K_PASS * g : K_PASS * (g + 1), cols].rearrange("(p t) l -> p t l", t=PACK)
-                nc.sync.dma_start(out=rows, in_=y_unit[unit][:])
+        def scale_row(dst, src, gain, on_vector):
+            if on_vector:
+                nc.vector.tensor_scalar(out=dst, in0=src, scalar1=gain, scalar2=None, op0=ALU.mult)
+            else:
+                nc.scalar.activation(out=dst, in_=src, func=ACT.Copy, scale=gain)
+
+        def store_y(n, halves=1):
+            unit, g, cols, h, width = half_of(n)
+            rows = out_0[K_PASS * g : K_PASS * (g + 1), cols].rearrange("(p t) l -> p t l", t=PACK)
+            slots = slice(2 * h, 2 * (h + halves))
+            nc.sync.dma_start(out=rows[:, slots, :], in_=y_unit[unit][:, slots, :])
+
+        def amplify(n, a, on_vector):
+            unit, g, cols, h, width = half_of(n)
+            t = 2 * h + a
+            scale_row(y_unit[unit][:, t, :], z_half[n][:, a, :], pow_f[:, g, t : t + 1], on_vector)
 
         def group_y(unit):
-            y_grouped[unit] = work.tile([P, CHUNK, PACK], BF16, name="y_grouped", align_bytes=64)
+            y_grouped[unit] = work.tile([P, UNITS[unit][2], PACK], BF16, name="y_grouped", bufs=3, align_bytes=64)
             interleave(y_grouped[unit][:], y_unit[unit][:])
 
         def quantize_y(unit):
-            g, c = divmod(unit, CHUNKS)
-            cols = slice(CHUNK * c, CHUNK * (c + 1))
+            g, lo, width = UNITS[unit]
+            cols = slice(lo, lo + width)
             nc.vector.quantize_mx(
                 out=y_codes[g][:, cols].bitcast(FP8X4),
-                scales=y_scales[g][:, cols],
+                scales=y_scales[:, g, cols],
                 in_=y_grouped[unit][:].rearrange("p l t -> p (l t)"),
             )
-            words = out_1[g].rearrange("p m t -> p (m t)").bitcast(I32)
-            nc.sync.dma_start(out=words[:, cols], in_=y_codes[g][:, cols].bitcast(I32))
-            if c == CHUNKS - 1:
-                for q in range(4):
-                    nc.sync.dma_start(
-                        out=out_2[g, 4 * q : 4 * q + 4, :].bitcast(I32),
-                        in_=y_scales[g][32 * q : 32 * q + 4, :].bitcast(I32),
-                    )
 
-        nc.vector.memset(cs_first[:].bitcast(I32), 0)
+        def store_words(g, lo, hi):
+            words = out_1[g].rearrange("p m t -> p (m t)").bitcast(I32)
+            nc.sync.dma_start(out=words[:, lo:hi], in_=y_codes[g][:, lo:hi].bitcast(I32))
+
+        def store_scales(lo, hi, queues):
+            for q in range(4):
+                queues[q].dma_start(
+                    out=out_2[lo:hi, 4 * q : 4 * q + 4, :].rearrange("g r m -> r g m").bitcast(I32),
+                    in_=y_scales[32 * q : 32 * q + 4, lo:hi, :].bitcast(I32),
+                )
+
         nc.vector.memset(bs[:].bitcast(I32), 0)
-        nc.vector.memset(cs_rest[:].bitcast(I32), 0)
+        nc.vector.memset(cs_raw[:].bitcast(I32), 0)
         nc.vector.memset(warm[:], 0.0)
         nc.scalar.activation(out=warm[:], in_=warm[:], func=ACT.Tanh)
         make_identity(nc, ident[:])
         load_c_words(0)
+        load_recode(0, parts=2)
         nc.sync.dma_start(out=bw[:].bitcast(I32), in_=b_words.rearrange("g p n -> p g n").bitcast(I32))
-        load_scale_rows(cs_first, c_scales[:, :, 0:K_PASS])
-        load_scale_rows(bs, b_scales)
-        load_recode(0)
+        load_scale_rows(nc.sync, cs_raw, c_scales)
+        load_scale_rows(nc.gpsimd, bs, b_scales)
         load_vector(att_b, att_f, att)
         load_vector(off_b, off_f, offset)
         load_recode(1)
-        load_scale_rows(cs_rest, c_scales[:, :, K_PASS:E])
         load_c_words(1)
         load_recode(2)
-        load_c_words(2)
         load_recode(3)
+        load_c_words(2)
+        load_recode(4)
         load_c_words(3)
-        for i in range(4, 8):
+        for i in range(5, 8):
             load_recode(i)
+
+        def turn(i):
+            turn_recode(i)
+            if i + 8 < T_GROUPS * PACK:
+                load_recode(i + 8)
+            if i == 1:
+                load_vector(pow_b, pow_f, power)
+                load_local(0)
+            if i == 3:
+                load_local(1)
+                load_local(2)
 
         order_c_words(0)
         order_c_scales(0)
-        code_pair(0, 0)
-        turn_recode(0)
-        load_recode(8)
-        order_c_words(1)
+        turn(0)
+        empty_turned(0, 0, False)
+        empty_turned(0, 1, False)
         order_c_scales(1)
-        code_pair(0, 1)
-        turn_recode(1)
-        load_recode(9)
-        load_vector(pow_b, pow_f, power)
-        load_local(0)
-        quantize_recode(0)
-        order_c_words(2)
+        code_pair(0, 0)
         order_c_scales(2)
-        for e in range(1, E_GROUPS + 1):
-            a, b, d = 3 * e - 1, 3 * e, 3 * e + 1
-            if e < E_GROUPS:
-                code_pair(e, 0)
-            turn_recode(a)
-            if e == 1:
-                load_recode(10)
-            group_received(e - 1, 0)
-            group_received(e - 1, 1)
-            quantize_received(e - 1, 0)
-            quantize_recode(a - 1)
-            quantize_received(e - 1, 1)
-            group_received(e - 1, 2)
-            if e < E_GROUPS:
-                turn_recode(b)
-                if e == 1:
-                    load_recode(11)
-                    load_local(1)
-                    load_local(2)
-                quantize_recode(a)
-                quantize_received(e - 1, 2)
-                code_pair(e, 1)
-                if e == 1:
-                    order_c_words(3)
-                    order_c_scales(3)
-                quantize_recode(b)
-                turn_recode(d)
-            else:
-                quantize_recode(a)
-                quantize_received(e - 1, 2)
-
-        halves = 2 * T_GROUPS * CHUNKS
-        for n in range(halves + 5):
-            if n < halves:
-                mix(n)
-                add_local(n)
-                limit(n)
-            if 1 <= n <= halves:
-                amplify(n - 1)
-            if n % 2 == 1 and 3 <= n < halves + 3:
-                group_y((n - 3) // 2)
-            if n % 2 == 0 and 4 <= n < halves + 4:
-                quantize_y((n - 4) // 2)
+        quantize_recode(0)
+        turn(1)
+        empty_turned(1, 0, False)
+        empty_turned(1, 1, False)
+        turn(2)
+        empty_turned(2, 0, False)
+        order_c_words(1)
+        code_pair(0, 1)
+        empty_turned(2, 1, True)
+        quantize_recode(1)
+        order_c_words(2)
+        group_received(0, 0)
+        group_received(0, 1)
+        quantize_received(0, 0)
+        code_pair(1, 0)
+        group_received(0, 2)
+        quantize_recode(2)
+        quantize_received(0, 1)
+        turn(3)
+        empty_turned(3, 0, False)
+        empty_turned(3, 1, False)
+        turn(4)
+        empty_turned(4, 0, False)
+        empty_turned(4, 1, False)
+        order_c_scales(3)
+        quantize_received(0, 2)
+        code_pair(1, 1)
+        quantize_recode(3)
+        order_c_words(3)
+        quantize_recode(4)
+        group_received(1, 0)
+        group_received(1, 1)
+        quantize_received(1, 0)
+        code_pair(2, 0)
+        group_received(1, 2)
+        quantize_received(1, 1)
+        turn(5)
+        empty_turned(5, 0, False)
+        empty_turned(5, 1, False)
+        turn(6)
+        empty_turned(6, 0, False)
+        quantize_received(1, 2)
+        empty_turned(6, 1, True)
+        code_pair(2, 1)
+        quantize_recode(5)
+        quantize_recode(6)
+        code_pair(3, 0)
+        group_received(2, 0)
+        group_received(2, 1)
+        quantize_received(2, 0)
+        turn(7)
+        empty_turned(7, 0, False)
+        empty_turned(7, 1, False)
+        turn(8)
+        empty_turned(8, 0, False)
+        group_received(2, 2)
+        quantize_received(2, 1)
+        empty_turned(8, 1, True)
+        quantize_received(2, 2)
+        code_pair(3, 1)
+        quantize_recode(7)
+        quantize_recode(8)
+        turn(9)
+        empty_turned(9, 0, False)
+        empty_turned(9, 1, False)
+        group_received(3, 0)
+        group_received(3, 1)
+        turn(10)
+        empty_turned(10, 0, False)
+        empty_turned(10, 1, False)
+        quantize_received(3, 0)
+        turn(11)
+        empty_turned(11, 0, False)
+        empty_turned(11, 1, False)
+        group_received(3, 2)
+        quantize_received(3, 1)
+        quantize_recode(9)
+        quantize_received(3, 2)
+        mix(0)
+        add_local(0)
+        limit(0)
+        mix(1)
+        add_local(1)
+        limit(1)
+        amplify(0, 0, False)
+        quantize_recode(10)
+        mix(2)
+        add_local(2)
+        amplify(0, 1, True)
+        store_y(0)
+        limit(2)
+        amplify(1, 0, False)
+        amplify(1, 1, False)
+        store_y(1)
+        quantize_recode(11)
+        mix(3)
+        add_local(3)
+        limit(3)
+        amplify(2, 0, False)
+        mix(4)
+        add_local(4)
+        amplify(2, 1, True)
+        store_y(2)
+        limit(4)
+        amplify(3, 0, False)
+        amplify(3, 1, False)
+        store_y(3)
+        group_y(0)
+        mix(5)
+        add_local(5)
+        limit(5)
+        amplify(4, 0, False)
+        quantize_y(0)
+        store_words(0, 0, 256)
+        mix(6)
+        add_local(6)
+        amplify(4, 1, True)
+        store_y(4)
+        limit(6)
+        amplify(5, 0, False)
+        amplify(5, 1, False)
+        store_y(5)
+        group_y(1)
+        mix(7)
+        add_local(7)
+        limit(7)
+        amplify(6, 0, False)
+        quantize_y(1)
+        store_words(0, 256, 512)
+        mix(8)
+        add_local(8)
+        amplify(6, 1, True)
+        store_y(6)
+        limit(8)
+        amplify(7, 0, False)
+        amplify(7, 1, False)
+        store_y(7)
+        group_y(2)
+        mix(9)
+        add_local(9)
+        limit(9)
+        amplify(8, 0, False)
+        quantize_y(2)
+        store_words(0, 512, 768)
+        mix(10)
+        add_local(10)
+        amplify(8, 1, True)
+        store_y(8)
+        limit(10)
+        amplify(9, 0, False)
+        amplify(9, 1, False)
+        store_y(9)
+        group_y(3)
+        mix(11)
+        add_local(11)
+        limit(11)
+        amplify(10, 0, False)
+        quantize_y(3)
+        store_words(1, 0, 256)
+        mix(12)
+        add_local(12)
+        amplify(10, 1, True)
+        store_y(10)
+        limit(12)
+        amplify(11, 0, False)
+        amplify(11, 1, False)
+        store_y(11)
+        group_y(4)
+        mix(13)
+        add_local(13)
+        limit(13)
+        amplify(12, 0, False)
+        quantize_y(4)
+        store_words(1, 256, 512)
+        mix(14)
+        add_local(14)
+        amplify(12, 1, True)
+        store_y(12)
+        limit(14)
+        amplify(13, 0, False)
+        amplify(13, 1, False)
+        store_y(13)
+        group_y(5)
+        mix(15)
+        add_local(15)
+        limit(15)
+        amplify(14, 0, False)
+        quantize_y(5)
+        store_words(1, 512, 768)
+        store_scales(0, 2, [nc.sync] * 4)
+        mix(16)
+        add_local(16)
+        amplify(14, 1, True)
+        store_y(14)
+        limit(16)
+        amplify(15, 0, False)
+        amplify(15, 1, False)
+        store_y(15)
+        group_y(6)
+        mix(17)
+        add_local(17)
+        limit(17)
+        quantize_y(6)
+        mix(18)
+        add_local(18)
+        amplify(16, 0, False)
+        amplify(16, 1, False)
+        amplify(17, 0, False)
+        amplify(17, 1, False)
+        store_y(16, halves=2)
+        group_y(7)
+        limit(18)
+        mix(19)
+        add_local(19)
+        limit(19)
+        quantize_y(7)
+        store_words(2, 0, 512)
+        group_y(8)
+        amplify(18, 0, False)
+        amplify(18, 1, False)
+        amplify(19, 0, True)
+        amplify(19, 1, False)
+        store_y(18, halves=2)
+        quantize_y(8)
+        group_y(9)
+        quantize_y(9)
+        store_words(2, 512, 768)
+        store_scales(2, 3, [nc.sync, nc.scalar, nc.sync, nc.scalar])

@@ -48,7 +48,8 @@ def tile_coded_relay_recode_k5_kernel(
         warm = kept("warm", [P, 1], F32)
         cw_raw = [kept("cw_raw%d" % e, [P, S_PASSES, 2 * K_PASS], U8) for e in range(E_GROUPS)]
         cw = [kept("cw%d" % e, [P, S_PASSES, PACK, 2 * P], U8) for e in range(E_GROUPS)]
-        cs_raw = kept("cs_raw", [P, S_PASSES, E], U8)
+        cs_first = kept("cs_first", [P, S_PASSES, K_PASS], U8)
+        cs_rest = kept("cs_rest", [P, S_PASSES, E - K_PASS], U8)
         cs = [kept("cs%d" % e, [P, S_PASSES, PACK, P], U8) for e in range(E_GROUPS)]
         bw = kept("bw", [P, S_PASSES, 2 * L], U8)
         bs = kept("bs", [P, S_PASSES, L], U8)
@@ -79,8 +80,8 @@ def tile_coded_relay_recode_k5_kernel(
         def new_bank():
             return psum.tile([P, BANK], F32, name="bank")
 
-        def load_scale_rows(queue, plane, rows):
-            for q in range(4):
+        def load_scale_rows(queue, plane, rows, quadrants=range(4)):
+            for q in quadrants:
                 queue.dma_start(
                     out=plane[32 * q : 32 * q + 4, :, :].bitcast(I32),
                     in_=rows[:, 4 * q : 4 * q + 4, :].rearrange("g r n -> r g n").bitcast(I32),
@@ -117,7 +118,7 @@ def tile_coded_relay_recode_k5_kernel(
             )
 
         def order_c_scales(e):
-            src = cs_raw[:, :, K_PASS * e : K_PASS * (e + 1)]
+            src = cs_first[:] if e == 0 else cs_rest[:, :, K_PASS * (e - 1) : K_PASS * e]
             nc.vector.tensor_copy(out=cs[e][:], in_=src.rearrange("p g (m t) -> p g t m", t=PACK))
 
         def turn_recode(i):
@@ -284,23 +285,26 @@ def tile_coded_relay_recode_k5_kernel(
                     in_=y_scales[32 * q : 32 * q + 4, lo:hi, :].bitcast(I32),
                 )
 
+        nc.vector.memset(cs_first[:].bitcast(I32), 0)
         nc.vector.memset(bs[:].bitcast(I32), 0)
-        nc.vector.memset(cs_raw[:].bitcast(I32), 0)
+        nc.vector.memset(cs_rest[:].bitcast(I32), 0)
         nc.vector.memset(warm[:], 0.0)
         nc.scalar.activation(out=warm[:], in_=warm[:], func=ACT.Tanh)
         make_identity(nc, ident[:])
         load_c_words(0)
-        load_recode(0, parts=2)
+        load_scale_rows(nc.sync, cs_first, c_scales[:, :, 0:K_PASS])
+        load_scale_rows(nc.sync, bs, b_scales, range(2))
         nc.sync.dma_start(out=bw[:].bitcast(I32), in_=b_words.rearrange("g p n -> p g n").bitcast(I32))
-        load_scale_rows(nc.sync, cs_raw, c_scales)
-        load_scale_rows(nc.gpsimd, bs, b_scales)
+        load_scale_rows(nc.sync, bs, b_scales, range(2, 4))
         load_vector(att_b, att_f, att)
         load_vector(off_b, off_f, offset)
-        load_recode(1)
         load_c_words(1)
+        load_scale_rows(nc.sync, cs_rest, c_scales[:, :, K_PASS:E])
+        load_recode(0)
+        load_recode(1)
+        load_c_words(2)
         load_recode(2)
         load_recode(3)
-        load_c_words(2)
         load_recode(4)
         load_c_words(3)
         for i in range(5, 8):
@@ -319,94 +323,94 @@ def tile_coded_relay_recode_k5_kernel(
 
         order_c_words(0)
         order_c_scales(0)
+        code_pair(0, 0)
+        order_c_words(1)
+        order_c_scales(1)
+        code_pair(0, 1)
+        order_c_scales(2)
+        order_c_scales(3)
         turn(0)
         empty_turned(0, 0, False)
         empty_turned(0, 1, False)
-        order_c_scales(1)
-        code_pair(0, 0)
-        order_c_scales(2)
-        quantize_recode(0)
         turn(1)
         empty_turned(1, 0, False)
-        empty_turned(1, 1, False)
-        turn(2)
-        empty_turned(2, 0, False)
-        order_c_words(1)
-        code_pair(0, 1)
-        empty_turned(2, 1, True)
-        quantize_recode(1)
-        order_c_words(2)
         group_received(0, 0)
         group_received(0, 1)
-        quantize_received(0, 0)
+        empty_turned(1, 1, True)
         code_pair(1, 0)
-        group_received(0, 2)
-        quantize_recode(2)
+        quantize_received(0, 0)
+        quantize_recode(0)
         quantize_received(0, 1)
+        group_received(0, 2)
+        quantize_recode(1)
+        quantize_received(0, 2)
+        turn(2)
+        empty_turned(2, 0, False)
+        empty_turned(2, 1, False)
         turn(3)
         empty_turned(3, 0, False)
-        empty_turned(3, 1, False)
-        turn(4)
-        empty_turned(4, 0, False)
-        empty_turned(4, 1, False)
-        order_c_scales(3)
-        quantize_received(0, 2)
+        order_c_words(2)
+        empty_turned(3, 1, True)
         code_pair(1, 1)
+        quantize_recode(2)
         quantize_recode(3)
         order_c_words(3)
-        quantize_recode(4)
+        code_pair(2, 0)
         group_received(1, 0)
         group_received(1, 1)
         quantize_received(1, 0)
-        code_pair(2, 0)
         group_received(1, 2)
         quantize_received(1, 1)
+        turn(4)
+        empty_turned(4, 0, False)
+        empty_turned(4, 1, False)
         turn(5)
         empty_turned(5, 0, False)
-        empty_turned(5, 1, False)
+        quantize_received(1, 2)
+        empty_turned(5, 1, True)
+        code_pair(2, 1)
+        quantize_recode(4)
+        quantize_recode(5)
         turn(6)
         empty_turned(6, 0, False)
-        quantize_received(1, 2)
-        empty_turned(6, 1, True)
-        code_pair(2, 1)
-        quantize_recode(5)
-        quantize_recode(6)
-        code_pair(3, 0)
+        empty_turned(6, 1, False)
         group_received(2, 0)
         group_received(2, 1)
         quantize_received(2, 0)
         turn(7)
         empty_turned(7, 0, False)
         empty_turned(7, 1, False)
-        turn(8)
-        empty_turned(8, 0, False)
         group_received(2, 2)
         quantize_received(2, 1)
-        empty_turned(8, 1, True)
+        code_pair(3, 0)
+        quantize_recode(6)
         quantize_received(2, 2)
-        code_pair(3, 1)
         quantize_recode(7)
-        quantize_recode(8)
+        turn(8)
+        empty_turned(8, 0, False)
+        empty_turned(8, 1, False)
         turn(9)
         empty_turned(9, 0, False)
-        empty_turned(9, 1, False)
-        group_received(3, 0)
-        group_received(3, 1)
+        empty_turned(9, 1, True)
+        code_pair(3, 1)
+        quantize_recode(8)
+        quantize_recode(9)
         turn(10)
         empty_turned(10, 0, False)
         empty_turned(10, 1, False)
+        group_received(3, 0)
+        group_received(3, 1)
         quantize_received(3, 0)
         turn(11)
         empty_turned(11, 0, False)
         empty_turned(11, 1, False)
         group_received(3, 2)
         quantize_received(3, 1)
-        quantize_recode(9)
-        quantize_received(3, 2)
         mix(0)
         add_local(0)
         limit(0)
         mix(1)
+        quantize_received(3, 2)
         add_local(1)
         limit(1)
         amplify(0, 0, False)

from contextlib import ExitStack

import concourse.mybir as mybir
from concourse.masks import make_identity

S, E, T, L = 1024, 2048, 1536, 768
FLOPS = 2 * S * E * L + 2 * T * E * L

F32 = mybir.dt.float32
BF16 = mybir.dt.bfloat16
I32 = mybir.dt.int32
U32 = mybir.dt.uint32
U8 = mybir.dt.uint8
FP8X4 = mybir.dt.float8_e4m3fn_x4
FP4X4 = mybir.dt.float4_e2m1fn_x4
ACT = mybir.ActivationFunctionType
ALU = mybir.AluOpType

P = 128
PACK = 4
K_PASS = P * PACK
S_PASSES = S // K_PASS
E_GROUPS = E // K_PASS
T_GROUPS = T // K_PASS
CHUNK = 256
CHUNKS = L // CHUNK
BANK = 512
UNITS = [(g, CHUNK * c, CHUNK) for g in range(T_GROUPS) for c in range(CHUNKS)][:-1]
UNITS = UNITS + [(T_GROUPS - 1, L - CHUNK, P), (T_GROUPS - 1, L - P, P)]


def tile_coded_relay_recode_k5_kernel(
    tc, c_words, c_scales, b_words, b_scales, att, offset, recode, local, power, out_0, out_1, out_2
):
    nc = tc.nc
    with ExitStack() as ctx:
        keep = ctx.enter_context(tc.tile_pool(name="keep", bufs=1))
        raw_pool = ctx.enter_context(tc.tile_pool(name="raw", bufs=8))
        work = ctx.enter_context(tc.tile_pool(name="work", bufs=2))
        ring = ctx.enter_context(tc.tile_pool(name="ring", bufs=4))
        psum = ctx.enter_context(tc.psum_pool(name="psum", bufs=8))
        ctx.enter_context(tc.manual_schedule())

        def kept(name, shape, dtype):
            return keep.tile(shape, dtype, name=name, align_bytes=64)

        ident = kept("ident", [P, P], F32)
        warm = kept("warm", [P, 1], F32)
        cw_raw = [kept("cw_raw%d" % e, [P, S_PASSES, 2 * K_PASS], U8) for e in range(E_GROUPS)]
        cw = [kept("cw%d" % e, [P, S_PASSES, PACK, 2 * P], U8) for e in range(E_GROUPS)]
        cs_first = kept("cs_first", [P, S_PASSES, K_PASS], U8)
        cs_rest = kept("cs_rest", [P, S_PASSES, E - K_PASS], U8)
        cs = [kept("cs%d" % e, [P, S_PASSES, PACK, P], U8) for e in range(E_GROUPS)]
        bw = kept("bw", [P, S_PASSES, 2 * L], U8)
        bs = kept("bs", [P, S_PASSES, L], U8)
        att_b = kept("att_b", [P, E_GROUPS, PACK], BF16)
        off_b = kept("off_b", [P, E_GROUPS, PACK], BF16)
        pow_b = kept("pow_b", [P, T_GROUPS, PACK], BF16)
        att_f = kept("att_f", [P, E_GROUPS, PACK], F32)
        off_f = kept("off_f", [P, E_GROUPS, PACK], F32)
        pow_f = kept("pow_f", [P, T_GROUPS, PACK], F32)
        loc = [kept("loc%d" % g, [P, PACK, L], BF16) for g in range(T_GROUPS)]
        rx_codes = [kept("rx_codes%d" % e, [P, L], U32) for e in range(E_GROUPS)]
        rx_scales = [kept("rx_scales%d" % e, [P, L], U8) for e in range(E_GROUPS)]
        w_codes = [kept("w_codes%d" % i, [P, E_GROUPS * P], U32) for i in range(T_GROUPS * PACK)]
        w_scales = [kept("w_scales%d" % i, [P, E_GROUPS * P], U8) for i in range(T_GROUPS * PACK)]
        y_codes = [kept("y_codes%d" % g, [P, L], U32) for g in range(T_GROUPS)]
        y_scales = kept("y_scales", [P, T_GROUPS, L], U8)

        turned = {}
        w_raw = {}
        w_grouped = {}
        rx_rows = {}
        rx_grouped = {}
        mix_bank = {}
        z_half = {}
        y_unit = {}
        y_grouped = {}

        def new_bank():
            return psum.tile([P, BANK], F32, name="bank")

        def load_scale_rows(queue, plane, rows, quadrants=range(4)):
            for q in quadrants:
                queue.dma_start(
                    out=plane[32 * q : 32 * q + 4, :, :].bitcast(I32),
                    in_=rows[:, 4 * q : 4 * q + 4, :].rearrange("g r n -> r g n").bitcast(I32),
                )

        def load_c_words(e):
            nc.sync.dma_start(
                out=cw_raw[e][:].bitcast(I32),
                in_=c_words[:, :, 2 * K_PASS * e : 2 * K_PASS * (e + 1)].rearrange("g p n -> p g n").bitcast(I32),
            )

        def load_recode(i, parts=1):
            g, j = divmod(i, PACK)
            w_raw[i] = raw_pool.tile([P, E], BF16, name="w_raw", align_bytes=64)
            rows = recode[K_PASS * g : K_PASS * (g + 1), :].rearrange("(m j) k -> m j k", j=PACK)
            width = E // parts
            for a in range(parts):
                cols = slice(width * a, width * (a + 1))
                nc.sync.dma_start(out=w_raw[i][:, cols], in_=rows[:, j, cols])

        def load_local(g):
            nc.sync.dma_start(
                out=loc[g][:], in_=local[K_PASS * g : K_PASS * (g + 1), :].rearrange("(p t) l -> p t l", t=PACK)
            )

        def load_vector(dst_b, dst_f, vec):
            nc.sync.dma_start(out=dst_b[:], in_=vec.rearrange("(g p t) -> p g t", p=P, t=PACK))
            nc.gpsimd.tensor_copy(out=dst_f[:], in_=dst_b[:])

        def order_c_words(e):
            nc.vector.tensor_copy(
                out=cw[e][:].rearrange("p g t (m b) -> p g t m b", b=2),
                in_=cw_raw[e][:].rearrange("p g (m t b) -> p g t m b", t=PACK, b=2),
            )

        def order_c_scales(e):
            src = cs_first[:] if e == 0 else cs_rest[:, :, K_PASS * (e - 1) : K_PASS * e]
            nc.vector.tensor_copy(out=cs[e][:], in_=src.rearrange("p g (m t) -> p g t m", t=PACK))

        def turn_recode(i):
            words = w_raw[i][:].bitcast(F32)
            for h in range(2):
                bank = new_bank()
                for a in range(2):
                    e = 2 * h + a
                    for u in range(2):
                        col = (2 * a + u) * P
                        nc.tensor.transpose(
                            bank[:, col : col + P], words[:, 2 * P * e + u : 2 * P * (e + 1) : 2], ident[:]
                        )
                turned[i, h] = bank

        def empty_turned(i, h, on_vector):
            if h == 0:
                w_grouped[i] = ring.tile([P, E_GROUPS, P, PACK], BF16, name="w_grouped", align_bytes=64)
            dst = w_grouped[i][:].bitcast(F32)[:, 2 * h : 2 * h + 2, :, :]
            src = turned[i, h][:].rearrange("p (a u m) -> p a m u", a=2, u=2)
            if on_vector:
                nc.vector.tensor_copy(out=dst, in_=src)
            else:
                nc.scalar.copy(out=dst, in_=src)

        def quantize_recode(i):
            nc.vector.quantize_mx(
                out=w_codes[i][:].bitcast(FP8X4),
                scales=w_scales[i][:],
                in_=w_grouped[i][:].rearrange("p e m t -> p (e m t)"),
            )

        def coded_passes(out, e, t, lo, hi):
            for g in range(S_PASSES):
                nc.tensor.matmul_mx(
                    out=out,
                    lhsT=cw[e][:, g, t, :].bitcast(FP4X4),
                    lhsT_scale=cs[e][:, g, t, :],
                    rhs=bw[:, g, 2 * lo : 2 * hi].bitcast(FP4X4),
                    rhs_scale=bs[:, g, lo:hi],
                    start=(g == 0),
                    stop=(g == S_PASSES - 1),
                )

        def receive(src, e, t, lo, hi):
            nc.scalar.activation(
                out=rx_rows[e][:, t, lo:hi],
                in_=src,
                func=ACT.Identity,
                bias=off_f[:, e, t : t + 1],
                scale=att_f[:, e, t : t + 1],
            )

        def code_pair(e, h):
            if h == 0:
                rx_rows[e] = work.tile([P, PACK, L], BF16, name="rx_rows", align_bytes=64)
            t0, t1 = 2 * h, 2 * h + 1
            rest = L - BANK
            first = new_bank()
            coded_passes(first[:], e, t0, 0, BANK)
            receive(first[:], e, t0, 0, BANK)
            second = new_bank()
            coded_passes(second[:], e, t1, 0, BANK)
            receive(second[:], e, t1, 0, BANK)
            shared = new_bank()
            coded_passes(shared[:, 0:rest], e, t0, BANK, L)
            coded_passes(shared[:, rest : 2 * rest], e, t1, BANK, L)
            receive(shared[:, 0:rest], e, t0, BANK, L)
            receive(shared[:, rest : 2 * rest], e, t1, BANK, L)

        def interleave(dst, src):
            nc.vector.tensor_copy(
                out=dst.rearrange("p (c i) t -> p c t i", i=4), in_=src.rearrange("p t (c i) -> p c t i", i=4)
            )

        def group_received(e, c):
            rx_grouped[e, c] = ring.tile([P, CHUNK, PACK], BF16, name="rx_grouped", align_bytes=64)
            interleave(rx_grouped[e, c][:], rx_rows[e][:, :, CHUNK * c : CHUNK * (c + 1)])

        def quantize_received(e, c):
            cols = slice(CHUNK * c, CHUNK * (c + 1))
            nc.vector.quantize_mx(
                out=rx_codes[e][:, cols].bitcast(FP8X4),
                scales=rx_scales[e][:, cols],
                in_=rx_grouped[e, c][:].rearrange("p l t -> p (l t)"),
            )

        def half_of(n):
            unit, h = divmod(n, 2)
            g, lo, width = UNITS[unit]
            return unit, g, slice(lo, lo + width), h, width

        def mix_passes(out, i, cols):
            for e in range(E_GROUPS):
                nc.tensor.matmul_mx(
                    out=out,
                    lhsT=w_codes[i][:, P * e : P * (e + 1)].bitcast(FP8X4),
                    lhsT_scale=w_scales[i][:, P * e : P * (e + 1)],
                    rhs=rx_codes[e][:, cols].bitcast(FP8X4),
                    rhs_scale=rx_scales[e][:, cols],
                    start=(e == 0),
                    stop=(e == E_GROUPS - 1),
                )

        def mix(n):
            unit, g, cols, h, width = half_of(n)
            mix_bank[n] = new_bank()
            for a in range(2):
                mix_passes(mix_bank[n][:, width * a : width * (a + 1)], PACK * g + 2 * h + a, cols)

        def add_local(n):
            unit, g, cols, h, width = half_of(n)
            if h == 0:
                y_unit[unit] = ring.tile([P, PACK, width], F32, name="y_unit")
            z_half[n] = ring.tile([P, 2, width], F32, name="z_half", bufs=6)
            nc.vector.tensor_tensor(
                out=z_half[n][:],
                in0=mix_bank[n][:, 0 : 2 * width].rearrange("p (a l) -> p a l", a=2),
                in1=loc[g][:, 2 * h : 2 * h + 2, cols],
                op=ALU.add,
            )

        def limit(n):
            nc.scalar.activation(out=z_half[n][:], in_=z_half[n][:], func=ACT.Tanh)

        def scale_row(dst, src, gain, on_vector):
            if on_vector:
                nc.vector.tensor_scalar(out=dst, in0=src, scalar1=gain, scalar2=None, op0=ALU.mult)
            else:
                nc.scalar.activation(out=dst, in_=src, func=ACT.Copy, scale=gain)

        def store_y(n, halves=1):
            unit, g, cols, h, width = half_of(n)
            rows = out_0[K_PASS * g : K_PASS * (g + 1), cols].rearrange("(p t) l -> p t l", t=PACK)
            slots = slice(2 * h, 2 * (h + halves))
            nc.sync.dma_start(out=rows[:, slots, :], in_=y_unit[unit][:, slots, :])

        def amplify(n, a, on_vector):
            unit, g, cols, h, width = half_of(n)
            t = 2 * h + a
            scale_row(y_unit[unit][:, t, :], z_half[n][:, a, :], pow_f[:, g, t : t + 1], on_vector)

        def group_y(unit):
            y_grouped[unit] = work.tile([P, UNITS[unit][2], PACK], BF16, name="y_grouped", bufs=3, align_bytes=64)
            interleave(y_grouped[unit][:], y_unit[unit][:])

        def quantize_y(unit):
            g, lo, width = UNITS[unit]
            cols = slice(lo, lo + width)
            nc.vector.quantize_mx(
                out=y_codes[g][:, cols].bitcast(FP8X4),
                scales=y_scales[:, g, cols],
                in_=y_grouped[unit][:].rearrange("p l t -> p (l t)"),
            )

        def store_words(g, lo, hi):
            words = out_1[g].rearrange("p m t -> p (m t)").bitcast(I32)
            nc.sync.dma_start(out=words[:, lo:hi], in_=y_codes[g][:, lo:hi].bitcast(I32))

        def store_scales(lo, hi, queues):
            for q in range(4):
                queues[q].dma_start(
                    out=out_2[lo:hi, 4 * q : 4 * q + 4, :].rearrange("g r m -> r g m").bitcast(I32),
                    in_=y_scales[32 * q : 32 * q + 4, lo:hi, :].bitcast(I32),
                )

        nc.vector.memset(cs_first[:].bitcast(I32), 0)
        nc.vector.memset(bs[:].bitcast(I32), 0)
        nc.vector.memset(cs_rest[:].bitcast(I32), 0)
        nc.vector.memset(warm[:], 0.0)
        nc.scalar.activation(out=warm[:], in_=warm[:], func=ACT.Tanh)
        make_identity(nc, ident[:])
        load_c_words(0)
        load_scale_rows(nc.sync, cs_first, c_scales[:, :, 0:K_PASS])
        load_scale_rows(nc.sync, bs, b_scales, range(2))
        nc.sync.dma_start(out=bw[:].bitcast(I32), in_=b_words.rearrange("g p n -> p g n").bitcast(I32))
        load_scale_rows(nc.sync, bs, b_scales, range(2, 4))
        load_vector(att_b, att_f, att)
        load_vector(off_b, off_f, offset)
        load_c_words(1)
        load_scale_rows(nc.sync, cs_rest, c_scales[:, :, K_PASS:E])
        load_recode(0)
        load_recode(1)
        load_c_words(2)
        load_recode(2)
        load_recode(3)
        load_recode(4)
        load_c_words(3)
        for i in range(5, 8):
            load_recode(i)

        def turn(i):
            turn_recode(i)
            if i + 8 < T_GROUPS * PACK:
                load_recode(i + 8)
            if i == 1:
                load_vector(pow_b, pow_f, power)
                load_local(0)
            if i == 3:
                load_local(1)
                load_local(2)

        order_c_words(0)
        order_c_scales(0)
        code_pair(0, 0)
        order_c_words(1)
        order_c_scales(1)
        code_pair(0, 1)
        order_c_scales(2)
        order_c_scales(3)
        turn(0)
        empty_turned(0, 0, False)
        empty_turned(0, 1, False)
        turn(1)
        empty_turned(1, 0, False)
        group_received(0, 0)
        group_received(0, 1)
        empty_turned(1, 1, True)
        code_pair(1, 0)
        quantize_received(0, 0)
        quantize_recode(0)
        quantize_received(0, 1)
        group_received(0, 2)
        quantize_recode(1)
        quantize_received(0, 2)
        turn(2)
        empty_turned(2, 0, False)
        empty_turned(2, 1, False)
        turn(3)
        empty_turned(3, 0, False)
        order_c_words(2)
        empty_turned(3, 1, True)
        code_pair(1, 1)
        quantize_recode(2)
        quantize_recode(3)
        order_c_words(3)
        code_pair(2, 0)
        group_received(1, 0)
        group_received(1, 1)
        quantize_received(1, 0)
        group_received(1, 2)
        quantize_received(1, 1)
        turn(4)
        empty_turned(4, 0, False)
        empty_turned(4, 1, False)
        turn(5)
        empty_turned(5, 0, False)
        quantize_received(1, 2)
        empty_turned(5, 1, True)
        code_pair(2, 1)
        quantize_recode(4)
        quantize_recode(5)
        turn(6)
        empty_turned(6, 0, False)
        empty_turned(6, 1, False)
        group_received(2, 0)
        group_received(2, 1)
        quantize_received(2, 0)
        turn(7)
        empty_turned(7, 0, False)
        empty_turned(7, 1, False)
        group_received(2, 2)
        quantize_received(2, 1)
        code_pair(3, 0)
        quantize_recode(6)
        quantize_received(2, 2)
        quantize_recode(7)
        turn(8)
        empty_turned(8, 0, False)
        empty_turned(8, 1, False)
        turn(9)
        empty_turned(9, 0, False)
        empty_turned(9, 1, True)
        code_pair(3, 1)
        quantize_recode(8)
        quantize_recode(9)
        turn(10)
        empty_turned(10, 0, False)
        empty_turned(10, 1, False)
        group_received(3, 0)
        group_received(3, 1)
        quantize_received(3, 0)
        turn(11)
        empty_turned(11, 0, False)
        empty_turned(11, 1, False)
        group_received(3, 2)
        quantize_received(3, 1)
        mix(0)
        add_local(0)
        limit(0)
        mix(1)
        quantize_received(3, 2)
        add_local(1)
        limit(1)
        amplify(0, 0, False)
        quantize_recode(10)
        mix(2)
        add_local(2)
        amplify(0, 1, True)
        store_y(0)
        limit(2)
        amplify(1, 0, False)
        amplify(1, 1, False)
        store_y(1)
        quantize_recode(11)
        mix(3)
        add_local(3)
        limit(3)
        amplify(2, 0, False)
        mix(4)
        add_local(4)
        amplify(2, 1, True)
        store_y(2)
        limit(4)
        amplify(3, 0, False)
        amplify(3, 1, False)
        store_y(3)
        group_y(0)
        mix(5)
        add_local(5)
        limit(5)
        amplify(4, 0, False)
        quantize_y(0)
        store_words(0, 0, 256)
        mix(6)
        add_local(6)
        amplify(4, 1, True)
        store_y(4)
        limit(6)
        amplify(5, 0, False)
        amplify(5, 1, False)
        store_y(5)
        group_y(1)
        mix(7)
        add_local(7)
        limit(7)
        amplify(6, 0, False)
        quantize_y(1)
        store_words(0, 256, 512)
        mix(8)
        add_local(8)
        amplify(6, 1, True)
        store_y(6)
        limit(8)
        amplify(7, 0, False)
        amplify(7, 1, False)
        store_y(7)
        group_y(2)
        mix(9)
        add_local(9)
        limit(9)
        amplify(8, 0, False)
        quantize_y(2)
        store_words(0, 512, 768)
        mix(10)
        add_local(10)
        amplify(8, 1, True)
        store_y(8)
        limit(10)
        amplify(9, 0, False)
        amplify(9, 1, False)
        store_y(9)
        group_y(3)
        mix(11)
        add_local(11)
        limit(11)
        amplify(10, 0, False)
        quantize_y(3)
        store_words(1, 0, 256)
        mix(12)
        add_local(12)
        amplify(10, 1, True)
        store_y(10)
        limit(12)
        amplify(11, 0, False)
        amplify(11, 1, False)
        store_y(11)
        group_y(4)
        mix(13)
        add_local(13)
        limit(13)
        amplify(12, 0, False)
        quantize_y(4)
        store_words(1, 256, 512)
        mix(14)
        add_local(14)
        amplify(12, 1, True)
        store_y(12)
        limit(14)
        amplify(13, 0, False)
        amplify(13, 1, False)
        store_y(13)
        group_y(5)
        mix(15)
        add_local(15)
        limit(15)
        amplify(14, 0, False)
        quantize_y(5)
        store_words(1, 512, 768)
        store_scales(0, 2, [nc.sync] * 4)
        mix(16)
        add_local(16)
        amplify(14, 1, True)
        store_y(14)
        limit(16)
        amplify(15, 0, False)
        amplify(15, 1, False)
        store_y(15)
        group_y(6)
        mix(17)
        add_local(17)
        limit(17)
        quantize_y(6)
        mix(18)
        add_local(18)
        amplify(16, 0, False)
        amplify(16, 1, False)
        amplify(17, 0, False)
        amplify(17, 1, False)
        store_y(16, halves=2)
        group_y(7)
        limit(18)
        mix(19)
        add_local(19)
        limit(19)
        quantize_y(7)
        store_words(2, 0, 512)
        group_y(8)
        amplify(18, 0, False)
        amplify(18, 1, False)
        amplify(19, 0, True)
        amplify(19, 1, False)
        store_y(18, halves=2)
        quantize_y(8)
        group_y(9)
        quantize_y(9)
        store_words(2, 512, 768)
        store_scales(2, 3, [nc.sync, nc.scalar, nc.sync, nc.scalar])
